import numpy as np
import ml_dtypes


def mxq(x, axis, fmt="e4m3"):
    dtype, down = {"e4m3": (ml_dtypes.float8_e4m3fn, 7), "e5m2": (ml_dtypes.float8_e5m2, 14)}[fmt]
    v = np.moveaxis(np.asarray(x, np.float32).astype(ml_dtypes.bfloat16).astype(np.float64), axis, -1)
    blocks = v.reshape(v.shape[:-1] + (-1, 32))
    amax = np.abs(blocks).max(-1, keepdims=True)
    byte = np.maximum(np.where(amax > 0, np.frexp(amax)[1] - 1 + 127, 0) - down, 1)
    scale = np.exp2(byte - 127.0)
    codes = (blocks / scale).astype(np.float32).astype(dtype).astype(np.float64)
    return np.moveaxis((codes * scale).reshape(v.shape), -1, axis)


WIDE = False


def mx_kscale(k):
    if not WIDE:
        return np.ones(k)
    levels = np.array([10, -10, 5, -5, 0])
    if k % 512:
        return np.exp2(np.random.permutation(np.resize(levels, k // 32))).repeat(32)
    a = np.empty((k // 512, 16))
    for p in range(k // 512):
        a[p, :8] = np.random.permutation(np.resize(levels, 8))
        for g in range(8):
            far = levels[np.abs(levels - a[p, g]) >= 10]
            a[p, g + 8] = far[np.random.randint(len(far))]
    return np.exp2(a.ravel()).repeat(32)


def f64(x):
    return np.asarray(x).astype(np.float64)


def striped(idx):
    return np.tile(np.asarray(idx).reshape(-1, 16).T, (8, 1)).astype(np.uint16)


def unstriped(offs):
    return offs[:16].T.reshape(-1).astype(np.int64)


E2M1 = np.array([0.0, 0.5, 1.0, 1.5, 2.0, 3.0, 4.0, 6.0, -0.0, -0.5, -1.0, -1.5, -2.0, -3.0, -4.0, -6.0])


def pack_weight(w, fmt):
    k, n = w.shape
    w = f64(np.asarray(w, np.float32).astype(ml_dtypes.bfloat16)).reshape(k // 32, 32, n)
    amax = np.abs(w).max(1)
    if fmt == "e4m3":
        byte = np.frexp(amax)[1] - 1 + 127 - 7
    else:
        mant, ex = np.frexp(amax / 6.0)
        byte = np.where(mant > 0.5, ex, ex - 1) + 127
    byte = np.clip(np.where(amax > 0, byte, 1), 1, 254)
    scaled = (w * np.exp2(127.0 - byte)[:, None, :]).reshape(k, n).astype(np.float32)
    by_word = np.ascontiguousarray(scaled.reshape(k // 512, 128, 4, n).transpose(0, 1, 3, 2))
    if fmt == "e4m3":
        words = by_word.astype(ml_dtypes.float8_e4m3fn).view(np.uint8)
    else:
        c = by_word.astype(ml_dtypes.float4_e2m1fn).view(np.uint8) & 0xF
        words = (c[..., 0::2] | (c[..., 1::2] << 4)).reshape(k // 512, 128, 2 * n)
    return np.ascontiguousarray(words), np.ascontiguousarray(byte.astype(np.uint8).reshape(k // 512, 16, n))


def unpack_weight(words, scales, fmt):
    g, _, n = scales.shape
    words = np.ascontiguousarray(words).reshape(g, 128, n, -1)
    if fmt == "e4m3":
        vals = words.view(ml_dtypes.float8_e4m3fn).astype(np.float64)
    else:
        nib = np.empty((g, 128, n, 4), np.uint8)
        nib[..., 0::2] = words & 0xF
        nib[..., 1::2] = words >> 4
        vals = E2M1[nib]
    vals = vals * np.repeat(np.exp2(scales.astype(np.float64) - 127.0), 8, axis=1)[..., None]
    return vals.transpose(0, 1, 3, 2).reshape(g * 512, n)


def sigmoid(v):
    return 1.0 / (1.0 + np.exp(-v))


K, T, J, N = 1024, 1024, 512, 512


def setup_inputs():
    n = np.random.standard_normal
    idx = np.random.permutation(T)[:J]
    idx2 = np.random.permutation(T)[:J]
    fk = mx_kscale(K)
    xtp = pack_weight(n((K, T)) / fk[:, None], "e4m3")
    wap = pack_weight(n((K, N)) * 1 / np.sqrt(K) * fk[:, None], "e2m1")
    return {
        "xt_words": xtp[0],
        "xt_scales": xtp[1],
        "wa_words": wap[0],
        "wa_scales": wap[1],
        "wb": (n((K, N)) * 1 / np.sqrt(K) * fk[:, None]).astype(np.float32),
        "res": (1.0 * n((N, T))).astype(np.float32),
        "offs": striped(idx),
        "offs2": striped(idx2),
    }


def reference(xt_words, xt_scales, wa_words, wa_scales, wb, res, offs, offs2):
    idx = unstriped(offs)
    idx2 = unstriped(offs2)
    xtu = unpack_weight(xt_words, xt_scales, "e4m3")
    wau = unpack_weight(wa_words, wa_scales, "e2m1")
    xtidxg = xtu[:, idx]
    a = wau.T @ xtidxg
    wbq = mxq(f64(wb), 0, "e4m3")
    xtidx2g = xtu[:, idx2]
    b = wbq.T @ xtidx2g
    d = a * sigmoid(b)
    dp = np.zeros((N, T))
    dp[:, idx] = d
    y = dp + 0.4 * f64(res)
    return y

@@ -1,0 +1,232 @@
+from contextlib import ExitStack
+
+import concourse.mybir as mybir
+
+K, T, J, N = 1024, 1024, 512, 512
+FLOPS = 2 * 2 * K * N * J
+
+F32 = mybir.dt.float32
+BF16 = mybir.dt.bfloat16
+I32 = mybir.dt.int32
+U32 = mybir.dt.uint32
+U16 = mybir.dt.uint16
+U8 = mybir.dt.uint8
+FP8X4 = mybir.dt.float8_e4m3fn_x4
+FP4X4 = mybir.dt.float4_e2m1fn_x4
+MULT = mybir.AluOpType.mult
+ADD = mybir.AluOpType.add
+SIGMOID = mybir.ActivationFunctionType.Sigmoid
+
+P = 128
+PACK = 4
+K_PASS = P * PACK
+PASSES = K // K_PASS
+BLOCKS = N // P
+HALF_N = N // 2
+HALF_J = J // 2
+LIST_COLS = J // 16
+RES_SCALE = 0.4
+SHIFT_ROWS = 112
+
+
+def tile_moe_one_expert_gates_another_kernel(tc, xt_words, xt_scales, wa_words, wa_scales, wb, res, offs, offs2, out):
+    nc = tc.nc
+    with ExitStack() as ctx:
+        keep = ctx.enter_context(tc.tile_pool(name="keep", bufs=1))
+        psum = ctx.enter_context(tc.psum_pool(name="psum", bufs=1))
+
+        def sb(name, shape, dtype, tag=""):
+            return keep.tile(shape, dtype, name=name, tag=tag or name, align_bytes=64)
+
+        list_a = keep.tile([P, LIST_COLS], U16, name="list_a")
+        list_b = keep.tile([P, LIST_COLS], U16, name="list_b")
+        x_words = [sb("x_words%d" % z, [P, T], I32) for z in range(PASSES)]
+        x_scales = sb("x_scales", [P, T], U8)
+        wa_codes = sb("wa_codes", [P, PASSES, 2 * N], U8)
+        wa_plane = sb("wa_plane", [P, PASSES, N], U8)
+        xa_shifted = sb("xa_shifted", [P, J], U8)
+        windows = [sb("window%d" % b, [P, T], F32) for b in range(2)]
+        warm = sb("warm", [P, 2], F32)
+
+        nc.vector.memset(x_scales[:].bitcast(I32), 0)
+        nc.vector.memset(wa_plane[:].rearrange("p z n -> p (z n)").bitcast(I32), 0)
+        nc.vector.memset(xa_shifted[:].bitcast(I32), 0)
+        nc.vector.memset(warm[:, 0:1], 0.0)
+
+        def words_src(z):
+            return xt_words[z].rearrange("p c r -> p (c r)").bitcast(I32)
+
+        wb_raw = {}
+
+        def load_wb(h):
+            for z in range(PASSES):
+                raw = sb("wb_raw%d%d" % (h, z), [P, PACK, HALF_N], F32, "wb_stage%d" % z)
+                rows = wb[z * K_PASS : (z + 1) * K_PASS, h * HALF_N : (h + 1) * HALF_N]
+                nc.sync.dma_start(raw[:], rows.rearrange("(p j) n -> p j n", j=PACK))
+                wb_raw[h, z] = raw
+
+        nc.sync.dma_start(list_b[:], offs2)
+        nc.sync.dma_start(x_words[0][:], words_src(0))
+        nc.sync.dma_start(list_a[:], offs)
+        nc.sync.dma_start(x_words[1][:], words_src(1))
+        load_wb(0)
+        for q in range(4):
+            nc.scalar.dma_start(
+                x_scales[32 * q : 32 * q + 8, :].bitcast(I32),
+                xt_scales[:, 4 * q : 4 * q + 4, :].bitcast(I32),
+            )
+        nc.scalar.dma_start(
+            wa_codes[:].bitcast(I32), wa_words.rearrange("z p c -> p z c").bitcast(I32)
+        )
+        for q in range(4):
+            nc.scalar.dma_start(
+                wa_plane[32 * q : 32 * q + 4, :, :].bitcast(I32),
+                wa_scales[:, 4 * q : 4 * q + 4, :].rearrange("z r n -> r z n").bitcast(I32),
+            )
+        nc.scalar.activation(warm[:, 1:2], warm[:, 0:1], SIGMOID)
+
+        for w in windows:
+            nc.vector.memset(w[:], 0.0)
+
+        xa_words = [sb("xa_words%d" % z, [P, J], U32) for z in range(PASSES)]
+        xb_words = {}
+        xa_scales = sb("xa_scales", [P, J], U8)
+        xb_scales = sb("xb_scales", [P, J], U8)
+
+        def gather_words(dst, z, lst, j0, j1):
+            nc.vector.tensor_copy(dst, x_words[z][:].bitcast(U32).indirect(lst[:, j0 // 16 : j1 // 16]))
+
+        wb_codes = {}
+        wb_scales = {}
+        wb_grouped = {}
+
+        def cast_wb(h, z):
+            grouped = sb("wb_grouped%d%d" % (h, z), [P, HALF_N, PACK], BF16)
+            nc.scalar.copy(
+                grouped[:].rearrange("p (c i) t -> p c t i", i=4),
+                wb_raw[h, z][:].rearrange("p t (c i) -> p c t i", i=4),
+            )
+            wb_grouped[h, z] = grouped
+
+        def quantize_wb(h, z):
+            codes = sb("wb_codes%d%d" % (h, z), [P, HALF_N], U32)
+            scales = sb("wb_scales%d%d" % (h, z), [P, HALF_N], U8)
+            nc.vector.quantize_mx(
+                out=codes[:].bitcast(FP8X4),
+                scales=scales[:],
+                in_=wb_grouped[h, z][:].rearrange("p n t -> p (n t)"),
+            )
+            wb_codes[h, z] = codes
+            wb_scales[h, z] = scales
+
+        cast_wb(0, 0)
+        cast_wb(0, 1)
+        xb_first = sb("xb_words0", [P, J], U32)
+        gather_words(xb_first[:], 0, list_b, 0, J)
+        xb_words[0, 0] = xb_first[:, 0:HALF_J]
+        xb_words[0, 1] = xb_first[:, HALF_J:J]
+        gather_words(xa_words[0][:], 0, list_a, 0, J)
+        nc.vector.tensor_copy(xa_scales[:], x_scales[:].indirect(list_a[:]))
+        nc.sync.dma_start(
+            xa_shifted[0:SHIFT_ROWS, :].bitcast(I32), xa_scales[4 : 4 + SHIFT_ROWS, :].bitcast(I32)
+        )
+        load_wb(1)
+        nc.vector.tensor_copy(xb_scales[:], x_scales[:].indirect(list_b[:]))
+        xb_low = sb("xb_words10", [P, HALF_J], U32)
+        gather_words(xb_low[:], 1, list_b, 0, HALF_J)
+        xb_words[1, 0] = xb_low[:]
+        gather_words(xa_words[1][:], 1, list_a, 0, J)
+        quantize_wb(0, 0)
+        quantize_wb(0, 1)
+        xb_high = sb("xb_words11", [P, HALF_J], U32, "wb_grouped01")
+        gather_words(xb_high[:], 1, list_b, HALF_J, J)
+        xb_words[1, 1] = xb_high[:]
+
+        res_tiles = {}
+
+        def load_res(b, tag):
+            r = sb("res%d" % b, [P, T], F32, tag)
+            nc.sync.dma_start(r[:], res[b * P : (b + 1) * P, :])
+            res_tiles[b] = r
+
+        load_res(0, "x_words0")
+
+        def gate_product(b, j0, j1, bank):
+            h, m0 = divmod(b * P, HALF_N)
+            acc = psum.tile([P, J], F32, name="acc", tag=bank)
+            for c0 in range(j0, j1, HALF_J):
+                for z in range(PASSES):
+                    nc.tensor.matmul_mx(
+                        out=acc[:, c0 - j0 : c0 - j0 + HALF_J],
+                        lhsT=wb_codes[h, z][:, m0 : m0 + P].bitcast(FP8X4),
+                        lhsT_scale=wb_scales[h, z][:, m0 : m0 + P],
+                        rhs=xb_words[z, c0 // HALF_J].bitcast(FP8X4),
+                        rhs_scale=xb_scales[4 * z : P, c0 : c0 + HALF_J],
+                        start=(z == 0),
+                        stop=(z == PASSES - 1),
+                    )
+            gate = sb("gate%d_%d" % (b, j0), [P, j1 - j0], F32)
+            nc.scalar.activation(gate[:], acc[:, 0 : j1 - j0], SIGMOID)
+            return gate
+
+        def value_product(b, j0, j1, bank, tag=""):
+            acc = psum.tile([P, J], F32, name="acc", tag=bank)
+            step = J if j1 - j0 == J else P
+            for c0 in range(j0, j1, step):
+                for z in range(PASSES):
+                    plane = xa_scales if z == 0 else xa_shifted
+                    nc.tensor.matmul_mx(
+                        out=acc[:, c0 - j0 : c0 - j0 + step],
+                        lhsT=wa_codes[:, z, 2 * b * P : 2 * (b + 1) * P].bitcast(FP4X4),
+                        lhsT_scale=wa_plane[:, z, b * P : (b + 1) * P],
+                        rhs=xa_words[z][:, c0 : c0 + step].bitcast(FP8X4),
+                        rhs_scale=plane[:, c0 : c0 + step],
+                        start=(z == 0),
+                        stop=(z == PASSES - 1),
+                    )
+            value = sb("value%d_%d" % (b, j0), [P, j1 - j0], F32, tag)
+            nc.scalar.copy(value[:], acc[:, 0 : j1 - j0])
+            return value
+
+        def scatter(b, j0, j1, value, gate):
+            nc.vector.tensor_tensor(
+                windows[b % 2][:].indirect(list_a[:, j0 // 16 : j1 // 16]), value[:], gate[:], MULT
+            )
+
+        def finish(b, pieces):
+            width = T // pieces
+            for c in range(pieces):
+                cols = slice(c * width, (c + 1) * width)
+                y = sb("y%d_%d" % (b, c), [P, width], F32)
+                nc.vector.scalar_tensor_tensor(
+                    y[:], res_tiles[b][:, cols], RES_SCALE, windows[b % 2][:, cols], MULT, ADD
+                )
+                queue = nc.sync if c % 2 == 0 else nc.scalar
+                queue.dma_start(out[b * P : (b + 1) * P, cols], y[:])
+
+        value = value_product(0, 0, HALF_J, "bank1")
+        gate = gate_product(0, 0, HALF_J, "bank0")
+        scatter(0, 0, HALF_J, value, gate)
+        load_res(1, "gate0_0")
+        gate = gate_product(0, HALF_J, J, "bank2")
+        value = value_product(0, HALF_J, J, "bank0")
+        scatter(0, HALF_J, J, value, gate)
+        gate = gate_product(1, 0, J, "bank3")
+        cast_wb(1, 0)
+        cast_wb(1, 1)
+        load_res(2, "wb_stage0")
+        value = value_product(1, 0, J, "bank2", "wb_stage1")
+        quantize_wb(1, 0)
+        quantize_wb(1, 1)
+        load_res(3, "wb_grouped11")
+        finish(0, 1)
+        scatter(1, 0, J, value, gate)
+        value = value_product(2, 0, J, "bank2")
+        gate = gate_product(2, 0, J, "bank3")
+        finish(1, 1)
+        scatter(2, 0, J, value, gate)
+        value = value_product(3, 0, J, "bank2")
+        gate = gate_product(3, 0, J, "bank0")
+        finish(2, 1)
+        scatter(3, 0, J, value, gate)
+        finish(3, 2)

@@ -33,6 +33,7 @@ def tile_moe_one_expert_gates_another_kernel(tc, xt_words, xt_scales, wa_words, 
     nc = tc.nc
     with ExitStack() as ctx:
         keep = ctx.enter_context(tc.tile_pool(name="keep", bufs=1))
+        shared = ctx.enter_context(tc.tile_pool(name="shared", bufs=1))
         psum = ctx.enter_context(tc.psum_pool(name="psum", bufs=1))
 
         def sb(name, shape, dtype, tag=""):
@@ -45,36 +46,37 @@ def tile_moe_one_expert_gates_another_kernel(tc, xt_words, xt_scales, wa_words, 
         wa_codes = sb("wa_codes", [P, PASSES, 2 * N], U8)
         wa_plane = sb("wa_plane", [P, PASSES, N], U8)
         xa_shifted = sb("xa_shifted", [P, J], U8)
-        windows = [sb("window%d" % b, [P, T], F32) for b in range(2)]
+        windows = [sb("window0", [P, T], F32)]
         warm = sb("warm", [P, 2], F32)
 
         nc.vector.memset(x_scales[:].bitcast(I32), 0)
-        nc.vector.memset(wa_plane[:].rearrange("p z n -> p (z n)").bitcast(I32), 0)
-        nc.vector.memset(xa_shifted[:].bitcast(I32), 0)
         nc.vector.memset(warm[:, 0:1], 0.0)
+        nc.vector.memset(xa_shifted[:].bitcast(I32), 0)
+        nc.vector.memset(wa_plane[:].rearrange("p z n -> p (z n)").bitcast(I32), 0)
+        nc.vector.memset(windows[0][:], 0.0)
 
         def words_src(z):
             return xt_words[z].rearrange("p c r -> p (c r)").bitcast(I32)
 
         wb_raw = {}
 
-        def load_wb(h):
-            for z in range(PASSES):
-                raw = sb("wb_raw%d%d" % (h, z), [P, PACK, HALF_N], F32, "wb_stage%d" % z)
-                rows = wb[z * K_PASS : (z + 1) * K_PASS, h * HALF_N : (h + 1) * HALF_N]
-                nc.sync.dma_start(raw[:], rows.rearrange("(p j) n -> p j n", j=PACK))
-                wb_raw[h, z] = raw
+        def load_wb(h, z, raw):
+            rows = wb[z * K_PASS : (z + 1) * K_PASS, h * HALF_N : (h + 1) * HALF_N]
+            nc.sync.dma_start(raw[:], rows.rearrange("(p j) n -> p j n", j=PACK))
+            wb_raw[h, z] = raw
 
-        nc.sync.dma_start(list_b[:], offs2)
-        nc.sync.dma_start(x_words[0][:], words_src(0))
         nc.sync.dma_start(list_a[:], offs)
-        nc.sync.dma_start(x_words[1][:], words_src(1))
-        load_wb(0)
+        nc.sync.dma_start(list_b[:], offs2)
         for q in range(4):
-            nc.scalar.dma_start(
+            queue = nc.sync if q < 2 else nc.scalar
+            queue.dma_start(
                 x_scales[32 * q : 32 * q + 8, :].bitcast(I32),
                 xt_scales[:, 4 * q : 4 * q + 4, :].bitcast(I32),
             )
+        for z in range(PASSES):
+            nc.sync.dma_start(x_words[z][:], words_src(z))
+            load_wb(0, z, sb("wb_raw0%d" % z, [P, PACK, HALF_N], F32))
+        nc.scalar.activation(warm[:, 1:2], warm[:, 0:1], SIGMOID)
         nc.scalar.dma_start(
             wa_codes[:].bitcast(I32), wa_words.rearrange("z p c -> p z c").bitcast(I32)
         )
@@ -83,10 +85,6 @@ def tile_moe_one_expert_gates_another_kernel(tc, xt_words, xt_scales, wa_words, 
                 wa_plane[32 * q : 32 * q + 4, :, :].bitcast(I32),
                 wa_scales[:, 4 * q : 4 * q + 4, :].rearrange("z r n -> r z n").bitcast(I32),
             )
-        nc.scalar.activation(warm[:, 1:2], warm[:, 0:1], SIGMOID)
-
-        for w in windows:
-            nc.vector.memset(w[:], 0.0)
 
         xa_words = [sb("xa_words%d" % z, [P, J], U32) for z in range(PASSES)]
         xb_words = {}
@@ -98,49 +96,49 @@ def tile_moe_one_expert_gates_another_kernel(tc, xt_words, xt_scales, wa_words, 
 
         wb_codes = {}
         wb_scales = {}
-        wb_grouped = {}
 
-        def cast_wb(h, z):
-            grouped = sb("wb_grouped%d%d" % (h, z), [P, HALF_N, PACK], BF16)
+        def cast_wb(h, z, grouped):
             nc.scalar.copy(
-                grouped[:].rearrange("p (c i) t -> p c t i", i=4),
+                grouped.rearrange("p (c i) t -> p c t i", i=4),
                 wb_raw[h, z][:].rearrange("p t (c i) -> p c t i", i=4),
             )
-            wb_grouped[h, z] = grouped
 
-        def quantize_wb(h, z):
-            codes = sb("wb_codes%d%d" % (h, z), [P, HALF_N], U32)
-            scales = sb("wb_scales%d%d" % (h, z), [P, HALF_N], U8)
+        def quantize_wb(h, passes, grouped):
+            width = len(passes) * HALF_N
+            codes = sb("wb_codes%d%d" % (h, passes[0]), [P, width], U32)
+            scales = sb("wb_scales%d%d" % (h, passes[0]), [P, width], U8)
             nc.vector.quantize_mx(
                 out=codes[:].bitcast(FP8X4),
                 scales=scales[:],
-                in_=wb_grouped[h, z][:].rearrange("p n t -> p (n t)"),
+                in_=grouped.rearrange("p n t -> p (n t)"),
             )
-            wb_codes[h, z] = codes
-            wb_scales[h, z] = scales
+            for i, z in enumerate(passes):
+                wb_codes[h, z] = codes[:, i * HALF_N : (i + 1) * HALF_N]
+                wb_scales[h, z] = scales[:, i * HALF_N : (i + 1) * HALF_N]
 
-        cast_wb(0, 0)
-        cast_wb(0, 1)
+        low = shared.tile([P, PASSES * HALF_N, PACK], BF16, name="wb_low", align_bytes=64, offset=3072)
+        nc.vector.tensor_copy(xa_scales[:], x_scales[:].indirect(list_a[:]))
+        nc.scalar.dma_start(
+            xa_shifted[0:SHIFT_ROWS, :].bitcast(I32), xa_scales[4 : 4 + SHIFT_ROWS, :].bitcast(I32)
+        )
+        cast_wb(0, 0, low[:, 0:HALF_N, :])
+        cast_wb(0, 1, low[:, HALF_N:, :])
+        nc.vector.tensor_copy(xb_scales[:], x_scales[:].indirect(list_b[:]))
+        gather_words(xa_words[0][:], 0, list_a, 0, J)
         xb_first = sb("xb_words0", [P, J], U32)
         gather_words(xb_first[:], 0, list_b, 0, J)
         xb_words[0, 0] = xb_first[:, 0:HALF_J]
         xb_words[0, 1] = xb_first[:, HALF_J:J]
-        gather_words(xa_words[0][:], 0, list_a, 0, J)
-        nc.vector.tensor_copy(xa_scales[:], x_scales[:].indirect(list_a[:]))
-        nc.sync.dma_start(
-            xa_shifted[0:SHIFT_ROWS, :].bitcast(I32), xa_scales[4 : 4 + SHIFT_ROWS, :].bitcast(I32)
-        )
-        load_wb(1)
-        nc.vector.tensor_copy(xb_scales[:], x_scales[:].indirect(list_b[:]))
+        gather_words(xa_words[1][:], 1, list_a, 0, J)
         xb_low = sb("xb_words10", [P, HALF_J], U32)
         gather_words(xb_low[:], 1, list_b, 0, HALF_J)
         xb_words[1, 0] = xb_low[:]
-        gather_words(xa_words[1][:], 1, list_a, 0, J)
-        quantize_wb(0, 0)
-        quantize_wb(0, 1)
-        xb_high = sb("xb_words11", [P, HALF_J], U32, "wb_grouped01")
+        quantize_wb(0, [0, 1], low[:])
+        xb_high = shared.tile([P, HALF_J], U32, name="xb_words11", align_bytes=64, offset=4096)
         gather_words(xb_high[:], 1, list_b, HALF_J, J)
         xb_words[1, 1] = xb_high[:]
+        windows.append(shared.tile([P, T], F32, name="window1", align_bytes=64, offset=5120))
+        nc.vector.memset(windows[1][:], 0.0)
 
         res_tiles = {}
 
@@ -150,6 +148,9 @@ def tile_moe_one_expert_gates_another_kernel(tc, xt_words, xt_scales, wa_words, 
             res_tiles[b] = r
 
         load_res(0, "x_words0")
+        load_res(2, "wb_raw00")
+        load_wb(1, 0, shared.tile([P, PACK, HALF_N], F32, name="wb_raw10", align_bytes=64, offset=0))
+        load_wb(1, 1, sb("wb_raw11", [P, PACK, HALF_N], F32, "x_words1"))
 
         def gate_product(b, j0, j1, bank):
             h, m0 = divmod(b * P, HALF_N)
@@ -169,64 +170,59 @@ def tile_moe_one_expert_gates_another_kernel(tc, xt_words, xt_scales, wa_words, 
             nc.scalar.activation(gate[:], acc[:, 0 : j1 - j0], SIGMOID)
             return gate
 
-        def value_product(b, j0, j1, bank, tag=""):
+        def value_product(b, bank, tag=""):
             acc = psum.tile([P, J], F32, name="acc", tag=bank)
-            step = J if j1 - j0 == J else P
-            for c0 in range(j0, j1, step):
-                for z in range(PASSES):
-                    plane = xa_scales if z == 0 else xa_shifted
-                    nc.tensor.matmul_mx(
-                        out=acc[:, c0 - j0 : c0 - j0 + step],
-                        lhsT=wa_codes[:, z, 2 * b * P : 2 * (b + 1) * P].bitcast(FP4X4),
-                        lhsT_scale=wa_plane[:, z, b * P : (b + 1) * P],
-                        rhs=xa_words[z][:, c0 : c0 + step].bitcast(FP8X4),
-                        rhs_scale=plane[:, c0 : c0 + step],
-                        start=(z == 0),
-                        stop=(z == PASSES - 1),
-                    )
-            value = sb("value%d_%d" % (b, j0), [P, j1 - j0], F32, tag)
-            nc.scalar.copy(value[:], acc[:, 0 : j1 - j0])
+            for z in range(PASSES):
+                plane = xa_scales if z == 0 else xa_shifted
+                nc.tensor.matmul_mx(
+                    out=acc[:],
+                    lhsT=wa_codes[:, z, 2 * b * P : 2 * (b + 1) * P].bitcast(FP4X4),
+                    lhsT_scale=wa_plane[:, z, b * P : (b + 1) * P],
+                    rhs=xa_words[z][:].bitcast(FP8X4),
+                    rhs_scale=plane[:],
+                    start=(z == 0),
+                    stop=(z == PASSES - 1),
+                )
+            value = sb("value%d" % b, [P, J], F32, tag)
+            nc.scalar.copy(value[:], acc[:])
             return value
 
         def scatter(b, j0, j1, value, gate):
             nc.vector.tensor_tensor(
-                windows[b % 2][:].indirect(list_a[:, j0 // 16 : j1 // 16]), value[:], gate[:], MULT
+                windows[b % 2][:].indirect(list_a[:, j0 // 16 : j1 // 16]), value[:, j0:j1], gate[:], MULT
             )
 
-        def finish(b, pieces):
-            width = T // pieces
-            for c in range(pieces):
-                cols = slice(c * width, (c + 1) * width)
-                y = sb("y%d_%d" % (b, c), [P, width], F32)
+        def finish(b, y, edges):
+            for c in range(len(edges) - 1):
+                cols = slice(edges[c], edges[c + 1])
                 nc.vector.scalar_tensor_tensor(
-                    y[:], res_tiles[b][:, cols], RES_SCALE, windows[b % 2][:, cols], MULT, ADD
+                    y[:, cols], res_tiles[b][:, cols], RES_SCALE, windows[b % 2][:, cols], MULT, ADD
                 )
                 queue = nc.sync if c % 2 == 0 else nc.scalar
-                queue.dma_start(out[b * P : (b + 1) * P, cols], y[:])
+                queue.dma_start(out[b * P : (b + 1) * P, cols], y[:, cols])
 
-        value = value_product(0, 0, HALF_J, "bank1")
+        value = value_product(0, "bank1", "wb_raw01")
         gate = gate_product(0, 0, HALF_J, "bank0")
         scatter(0, 0, HALF_J, value, gate)
         load_res(1, "gate0_0")
-        gate = gate_product(0, HALF_J, J, "bank2")
-        value = value_product(0, HALF_J, J, "bank0")
+        gate = gate_product(0, HALF_J, J, "bank3")
         scatter(0, HALF_J, J, value, gate)
-        gate = gate_product(1, 0, J, "bank3")
-        cast_wb(1, 0)
-        cast_wb(1, 1)
-        load_res(2, "wb_stage0")
-        value = value_product(1, 0, J, "bank2", "wb_stage1")
-        quantize_wb(1, 0)
-        quantize_wb(1, 1)
-        load_res(3, "wb_grouped11")
-        finish(0, 1)
+        load_res(3, "gate0_256")
+        gate = gate_product(1, 0, J, "bank4")
+        value = value_product(1, "bank0")
         scatter(1, 0, J, value, gate)
-        value = value_product(2, 0, J, "bank2")
-        gate = gate_product(2, 0, J, "bank3")
-        finish(1, 1)
+        high = sb("wb_high", [P, PASSES * HALF_N, PACK], BF16)
+        cast_wb(1, 0, high[:, 0:HALF_N, :])
+        cast_wb(1, 1, high[:, HALF_N:, :])
+        quantize_wb(1, [0, 1], high[:])
+        value = value_product(2, "bank0", "x_words1")
+        gate = gate_product(2, 0, J, "bank1")
+        y_pair = sb("y01", [P, 2 * T], F32, "wb_high")
+        finish(0, y_pair[:, 0:T], (0, T))
+        finish(1, y_pair[:, T:], (0, T))
         scatter(2, 0, J, value, gate)
-        value = value_product(3, 0, J, "bank2")
-        gate = gate_product(3, 0, J, "bank0")
-        finish(2, 1)
+        gate = gate_product(3, 0, J, "bank2")
+        value = value_product(3, "bank0")
+        finish(2, sb("y2", [P, T], F32), (0, T))
         scatter(3, 0, J, value, gate)
-        finish(3, 2)
+        finish(3, sb("y3", [P, T], F32), (0, T // 2, 3 * T // 4, T))

@@ -1,6 +1,7 @@
 from contextlib import ExitStack
 
 import concourse.mybir as mybir
+from concourse.masks import make_identity
 
 K, T, J, N = 1024, 1024, 512, 512
 FLOPS = 2 * 2 * K * N * J
@@ -33,6 +34,7 @@ def tile_moe_one_expert_gates_another_kernel(tc, xt_words, xt_scales, wa_words, 
     nc = tc.nc
     with ExitStack() as ctx:
         keep = ctx.enter_context(tc.tile_pool(name="keep", bufs=1))
+        later = ctx.enter_context(tc.tile_pool(name="later", bufs=1))
         shared = ctx.enter_context(tc.tile_pool(name="shared", bufs=1))
         psum = ctx.enter_context(tc.psum_pool(name="psum", bufs=1))
 
@@ -46,24 +48,28 @@ def tile_moe_one_expert_gates_another_kernel(tc, xt_words, xt_scales, wa_words, 
         wa_codes = sb("wa_codes", [P, PASSES, 2 * N], U8)
         wa_plane = sb("wa_plane", [P, PASSES, N], U8)
         xa_shifted = sb("xa_shifted", [P, J], U8)
-        windows = [sb("window0", [P, T], F32)]
+        windows = [sb("window%d" % b, [P, T], F32) for b in range(2)]
+        identity = sb("identity", [P, P], F32)
         warm = sb("warm", [P, 2], F32)
 
         nc.vector.memset(x_scales[:].bitcast(I32), 0)
         nc.vector.memset(warm[:, 0:1], 0.0)
         nc.vector.memset(xa_shifted[:].bitcast(I32), 0)
         nc.vector.memset(wa_plane[:].rearrange("p z n -> p (z n)").bitcast(I32), 0)
-        nc.vector.memset(windows[0][:], 0.0)
+        nc.vector.memset(identity[:], 0.0)
+        make_identity(nc, identity[:], nomemset=True)
+        for w in windows:
+            nc.vector.memset(w[:], 0.0)
 
         def words_src(z):
             return xt_words[z].rearrange("p c r -> p (c r)").bitcast(I32)
 
         wb_raw = {}
 
-        def load_wb(h, z, raw):
-            rows = wb[z * K_PASS : (z + 1) * K_PASS, h * HALF_N : (h + 1) * HALF_N]
+        def load_wb(b, z, raw):
+            rows = wb[z * K_PASS : (z + 1) * K_PASS, b * P : b * P + raw.shape[2]]
             nc.sync.dma_start(raw[:], rows.rearrange("(p j) n -> p j n", j=PACK))
-            wb_raw[h, z] = raw
+            wb_raw[b, z] = raw
 
         nc.sync.dma_start(list_a[:], offs)
         nc.sync.dma_start(list_b[:], offs2)
@@ -73,9 +79,10 @@ def tile_moe_one_expert_gates_another_kernel(tc, xt_words, xt_scales, wa_words, 
                 x_scales[32 * q : 32 * q + 8, :].bitcast(I32),
                 xt_scales[:, 4 * q : 4 * q + 4, :].bitcast(I32),
             )
+        nc.sync.dma_start(x_words[0][:], words_src(0))
         for z in range(PASSES):
-            nc.sync.dma_start(x_words[z][:], words_src(z))
             load_wb(0, z, sb("wb_raw0%d" % z, [P, PACK, HALF_N], F32))
+        nc.sync.dma_start(x_words[1][:], words_src(1))
         nc.scalar.activation(warm[:, 1:2], warm[:, 0:1], SIGMOID)
         nc.scalar.dma_start(
             wa_codes[:].bitcast(I32), wa_words.rearrange("z p c -> p z c").bitcast(I32)
@@ -87,7 +94,7 @@ def tile_moe_one_expert_gates_another_kernel(tc, xt_words, xt_scales, wa_words, 
             )
 
         xa_words = [sb("xa_words%d" % z, [P, J], U32) for z in range(PASSES)]
-        xb_words = {}
+        xb_words = [sb("xb_words%d" % z, [P, J], U32) for z in range(PASSES)]
         xa_scales = sb("xa_scales", [P, J], U8)
         xb_scales = sb("xb_scales", [P, J], U8)
 
@@ -97,48 +104,43 @@ def tile_moe_one_expert_gates_another_kernel(tc, xt_words, xt_scales, wa_words, 
         wb_codes = {}
         wb_scales = {}
 
-        def cast_wb(h, z, grouped):
-            nc.scalar.copy(
-                grouped.rearrange("p (c i) t -> p c t i", i=4),
-                wb_raw[h, z][:].rearrange("p t (c i) -> p c t i", i=4),
-            )
+        def cast_wb(b, grouped):
+            width = grouped.shape[1] // PASSES
+            for z in range(PASSES):
+                nc.scalar.copy(
+                    grouped[:, z * width : (z + 1) * width, :].rearrange("p (c i) t -> p c t i", i=4),
+                    wb_raw[b, z][:].rearrange("p t (c i) -> p c t i", i=4),
+                )
 
-        def quantize_wb(h, passes, grouped):
-            width = len(passes) * HALF_N
-            codes = sb("wb_codes%d%d" % (h, passes[0]), [P, width], U32)
-            scales = sb("wb_scales%d%d" % (h, passes[0]), [P, width], U8)
+        def quantize_wb(b, grouped):
+            words = grouped.shape[1]
+            width = words // PASSES
+            codes = sb("wb_codes%d" % b, [P, words], U32)
+            scales = sb("wb_scales%d" % b, [P, words], U8)
             nc.vector.quantize_mx(
                 out=codes[:].bitcast(FP8X4),
                 scales=scales[:],
-                in_=grouped.rearrange("p n t -> p (n t)"),
+                in_=grouped[:].rearrange("p n t -> p (n t)"),
             )
-            for i, z in enumerate(passes):
-                wb_codes[h, z] = codes[:, i * HALF_N : (i + 1) * HALF_N]
-                wb_scales[h, z] = scales[:, i * HALF_N : (i + 1) * HALF_N]
+            for i in range(width // P):
+                for z in range(PASSES):
+                    cols = slice(z * width + i * P, z * width + (i + 1) * P)
+                    wb_codes[b + i, z] = codes[:, cols]
+                    wb_scales[b + i, z] = scales[:, cols]
 
         low = shared.tile([P, PASSES * HALF_N, PACK], BF16, name="wb_low", align_bytes=64, offset=3072)
         nc.vector.tensor_copy(xa_scales[:], x_scales[:].indirect(list_a[:]))
         nc.scalar.dma_start(
             xa_shifted[0:SHIFT_ROWS, :].bitcast(I32), xa_scales[4 : 4 + SHIFT_ROWS, :].bitcast(I32)
         )
-        cast_wb(0, 0, low[:, 0:HALF_N, :])
-        cast_wb(0, 1, low[:, HALF_N:, :])
+        cast_wb(0, low)
         nc.vector.tensor_copy(xb_scales[:], x_scales[:].indirect(list_b[:]))
         gather_words(xa_words[0][:], 0, list_a, 0, J)
-        xb_first = sb("xb_words0", [P, J], U32)
-        gather_words(xb_first[:], 0, list_b, 0, J)
-        xb_words[0, 0] = xb_first[:, 0:HALF_J]
-        xb_words[0, 1] = xb_first[:, HALF_J:J]
-        gather_words(xa_words[1][:], 1, list_a, 0, J)
-        xb_low = sb("xb_words10", [P, HALF_J], U32)
-        gather_words(xb_low[:], 1, list_b, 0, HALF_J)
-        xb_words[1, 0] = xb_low[:]
-        quantize_wb(0, [0, 1], low[:])
-        xb_high = shared.tile([P, HALF_J], U32, name="xb_words11", align_bytes=64, offset=4096)
-        gather_words(xb_high[:], 1, list_b, HALF_J, J)
-        xb_words[1, 1] = xb_high[:]
-        windows.append(shared.tile([P, T], F32, name="window1", align_bytes=64, offset=5120))
-        nc.vector.memset(windows[1][:], 0.0)
+        gather_words(xb_words[0][:], 0, list_b, 0, J)
+        quantize_wb(0, low)
+        for j0 in (0, HALF_J):
+            gather_words(xb_words[1][:, j0 : j0 + HALF_J], 1, list_b, j0, j0 + HALF_J)
+            gather_words(xa_words[1][:, j0 : j0 + HALF_J], 1, list_a, j0, j0 + HALF_J)
 
         res_tiles = {}
 
@@ -148,81 +150,130 @@ def tile_moe_one_expert_gates_another_kernel(tc, xt_words, xt_scales, wa_words, 
             res_tiles[b] = r
 
         load_res(0, "x_words0")
-        load_res(2, "wb_raw00")
-        load_wb(1, 0, shared.tile([P, PACK, HALF_N], F32, name="wb_raw10", align_bytes=64, offset=0))
-        load_wb(1, 1, sb("wb_raw11", [P, PACK, HALF_N], F32, "x_words1"))
+        load_res(1, "wb_raw00")
+        load_wb(2, 0, shared.tile([P, PACK, P], F32, name="wb_raw20", align_bytes=64, offset=2048))
+        load_wb(2, 1, sb("wb_raw21", [P, PACK, P], F32, "x_words1"))
 
-        def gate_product(b, j0, j1, bank):
-            h, m0 = divmod(b * P, HALF_N)
-            acc = psum.tile([P, J], F32, name="acc", tag=bank)
-            for c0 in range(j0, j1, HALF_J):
-                for z in range(PASSES):
-                    nc.tensor.matmul_mx(
-                        out=acc[:, c0 - j0 : c0 - j0 + HALF_J],
-                        lhsT=wb_codes[h, z][:, m0 : m0 + P].bitcast(FP8X4),
-                        lhsT_scale=wb_scales[h, z][:, m0 : m0 + P],
-                        rhs=xb_words[z, c0 // HALF_J].bitcast(FP8X4),
-                        rhs_scale=xb_scales[4 * z : P, c0 : c0 + HALF_J],
-                        start=(z == 0),
-                        stop=(z == PASSES - 1),
-                    )
-            gate = sb("gate%d_%d" % (b, j0), [P, j1 - j0], F32)
-            nc.scalar.activation(gate[:], acc[:, 0 : j1 - j0], SIGMOID)
-            return gate
-
-        def value_product(b, bank, tag=""):
+        def gate_product(b, j0, j1, bank, gate):
             acc = psum.tile([P, J], F32, name="acc", tag=bank)
             for z in range(PASSES):
-                plane = xa_scales if z == 0 else xa_shifted
                 nc.tensor.matmul_mx(
-                    out=acc[:],
-                    lhsT=wa_codes[:, z, 2 * b * P : 2 * (b + 1) * P].bitcast(FP4X4),
-                    lhsT_scale=wa_plane[:, z, b * P : (b + 1) * P],
-                    rhs=xa_words[z][:].bitcast(FP8X4),
-                    rhs_scale=plane[:],
+                    out=acc[:, 0 : j1 - j0],
+                    lhsT=wb_codes[b, z].bitcast(FP8X4),
+                    lhsT_scale=wb_scales[b, z],
+                    rhs=xb_words[z][:, j0:j1].bitcast(FP8X4),
+                    rhs_scale=xb_scales[4 * z : P, j0:j1],
                     start=(z == 0),
                     stop=(z == PASSES - 1),
                 )
-            value = sb("value%d" % b, [P, J], F32, tag)
-            nc.scalar.copy(value[:], acc[:])
-            return value
+            nc.scalar.activation(gate, acc[:, 0 : j1 - j0], SIGMOID)
+
+        def value_product(b, j0, j1, bank, value):
+            acc = psum.tile([P, J], F32, name="acc", tag=bank)
+            step = J if j1 - j0 == J else P
+            for c0 in range(j0, j1, step):
+                for z in range(PASSES):
+                    plane = xa_scales if z == 0 else xa_shifted
+                    nc.tensor.matmul_mx(
+                        out=acc[:, c0 - j0 : c0 - j0 + step],
+                        lhsT=wa_codes[:, z, 2 * b * P : 2 * (b + 1) * P].bitcast(FP4X4),
+                        lhsT_scale=wa_plane[:, z, b * P : (b + 1) * P],
+                        rhs=xa_words[z][:, c0 : c0 + step].bitcast(FP8X4),
+                        rhs_scale=plane[:, c0 : c0 + step],
+                        start=(z == 0),
+                        stop=(z == PASSES - 1),
+                    )
+            if b < 2:
+                nc.scalar.mul(value, acc[:, 0 : j1 - j0], 1.0 / RES_SCALE)
+            else:
+                nc.scalar.copy(value, acc[:, 0 : j1 - j0])
 
         def scatter(b, j0, j1, value, gate):
             nc.vector.tensor_tensor(
-                windows[b % 2][:].indirect(list_a[:, j0 // 16 : j1 // 16]), value[:, j0:j1], gate[:], MULT
+                windows[b % 3][:].indirect(list_a[:, j0 // 16 : j1 // 16]), value, gate, MULT
             )
 
         def finish(b, y, edges):
             for c in range(len(edges) - 1):
                 cols = slice(edges[c], edges[c + 1])
                 nc.vector.scalar_tensor_tensor(
-                    y[:, cols], res_tiles[b][:, cols], RES_SCALE, windows[b % 2][:, cols], MULT, ADD
+                    y[:, cols], res_tiles[b][:, cols], RES_SCALE, windows[b % 3][:, cols], MULT, ADD
                 )
-                queue = nc.sync if c % 2 == 0 else nc.scalar
-                queue.dma_start(out[b * P : (b + 1) * P, cols], y[:, cols])
+                nc.sync.dma_start(out[b * P : (b + 1) * P, cols], y[:, cols])
 
-        value = value_product(0, "bank1", "wb_raw01")
-        gate = gate_product(0, 0, HALF_J, "bank0")
-        scatter(0, 0, HALF_J, value, gate)
-        load_res(1, "gate0_0")
-        gate = gate_product(0, HALF_J, J, "bank3")
-        scatter(0, HALF_J, J, value, gate)
-        load_res(3, "gate0_256")
-        gate = gate_product(1, 0, J, "bank4")
-        value = value_product(1, "bank0")
-        scatter(1, 0, J, value, gate)
-        high = sb("wb_high", [P, PASSES * HALF_N, PACK], BF16)
-        cast_wb(1, 0, high[:, 0:HALF_N, :])
-        cast_wb(1, 1, high[:, HALF_N:, :])
-        quantize_wb(1, [0, 1], high[:])
-        value = value_product(2, "bank0", "x_words1")
-        gate = gate_product(2, 0, J, "bank1")
-        y_pair = sb("y01", [P, 2 * T], F32, "wb_high")
-        finish(0, y_pair[:, 0:T], (0, T))
-        finish(1, y_pair[:, T:], (0, T))
-        scatter(2, 0, J, value, gate)
-        gate = gate_product(3, 0, J, "bank2")
-        value = value_product(3, "bank0")
+        def add_turned(b, half, bank, staged):
+            turned = psum.tile([P, J], F32, name="acc", tag=bank)
+            for c in range(J // P):
+                cols = slice(half * J + c * P, half * J + (c + 1) * P)
+                for source, first in ((res_tiles[b], True), (windows[b % 3], False)):
+                    nc.tensor.matmul(
+                        turned[:, c * P : (c + 1) * P],
+                        lhsT=source[:, cols],
+                        rhs=identity[:],
+                        start=first,
+                        stop=not first,
+                        is_transpose=True,
+                    )
+            nc.scalar.copy(staged, turned[:])
+
+        def turn_back(b, half, bank, staged):
+            back = psum.tile([P, J], F32, name="acc", tag=bank)
+            for c in range(J // P):
+                cols = slice(c * P, (c + 1) * P)
+                nc.tensor.transpose(back[:, cols], staged[:, cols], identity[:])
+            y = sb("y%d_%d" % (b, half), [P, J], F32)
+            nc.scalar.mul(y[:], back[:], RES_SCALE)
+            nc.scalar.dma_start(out[b * P : (b + 1) * P, half * J : (half + 1) * J], y[:])
+
+        value = sb("value0_0", [P, HALF_J], F32)
+        gate = later.tile([P, HALF_J], F32, name="gate0_0", align_bytes=64, offset=1536)
+        gate_product(0, 0, HALF_J, "bank0", gate[:])
+        value_product(0, 0, HALF_J, "bank1", value[:])
+        scatter(0, 0, HALF_J, value[:], gate[:])
+        windows.append(sb("window2", [P, T], F32, "value0_0"))
+        nc.gpsimd.memset(windows[2][:], 0.0)
+        for z in range(PASSES):
+            load_wb(3, z, later.tile([P, PACK, P], F32, name="wb_raw3%d" % z, align_bytes=64, offset=2048 * z))
+        gate = sb("gate0_256", [P, HALF_J], F32)
+        gate_product(0, HALF_J, J, "bank3", gate[:])
+        value = sb("value0_256", [P, HALF_J], F32, "wb_raw01")
+        value_product(0, HALF_J, J, "bank5", value[:])
+        scatter(0, HALF_J, J, value[:], gate[:])
+        load_res(2, "wb_raw01")
+
+        gate = sb("gate1", [P, J], F32)
+        gate_product(1, 0, J, "bank4", gate[:])
+        grouped = sb("wb_third", [P, PASSES * P, PACK], BF16)
+        cast_wb(2, grouped)
+        value = sb("value1", [P, J], F32, "x_words1")
+        value_product(1, 0, J, "bank6", value[:])
+        quantize_wb(2, grouped)
+        scatter(1, 0, J, value[:], gate[:])
+        load_res(3, "x_words1")
+
+        gate = sb("gate2", [P, J], F32)
+        gate_product(2, 0, J, "bank1", gate[:])
+        grouped = sb("wb_fourth", [P, PASSES * P, PACK], BF16)
+        cast_wb(3, grouped)
+        value = later.tile([P, J], F32, name="value2", align_bytes=64, offset=2048)
+        value_product(2, 0, J, "bank7", value[:])
+        quantize_wb(3, grouped)
+        scatter(2, 0, J, value[:], gate[:])
+
+        late = sb("late", [P, 3 * J], F32, "wb_fourth")
+        value = late[:, 0:J]
+        value_product(3, 0, J, "bank0", value)
+        add_turned(0, 0, "bank6", late[:, J : 2 * J])
+        add_turned(0, 1, "bank1", late[:, 2 * J : 3 * J])
+        gate = sb("gate3", [P, J], F32)
+        gate_product(3, 0, J, "bank2", gate[:])
+        turn_back(0, 0, "bank6", late[:, J : 2 * J])
+        turn_back(0, 1, "bank1", late[:, 2 * J : 3 * J])
         finish(2, sb("y2", [P, T], F32), (0, T))
-        scatter(3, 0, J, value, gate)
+        scatter(3, 0, J, value, gate[:])
+        staged = sb("staged1", [P, T], F32)
+        add_turned(1, 0, "bank0", staged[:, 0:J])
+        add_turned(1, 1, "bank2", staged[:, J:T])
+        turn_back(1, 0, "bank0", staged[:, 0:J])
+        turn_back(1, 1, "bank2", staged[:, J:T])
         finish(3, sb("y3", [P, T], F32), (0, T // 2, 3 * T // 4, T))

from contextlib import ExitStack

import concourse.mybir as mybir
from concourse.masks import make_identity

K, T, J, N = 1024, 1024, 512, 512
FLOPS = 2 * 2 * K * N * J

F32 = mybir.dt.float32
BF16 = mybir.dt.bfloat16
I32 = mybir.dt.int32
U32 = mybir.dt.uint32
U16 = mybir.dt.uint16
U8 = mybir.dt.uint8
FP8X4 = mybir.dt.float8_e4m3fn_x4
FP4X4 = mybir.dt.float4_e2m1fn_x4
MULT = mybir.AluOpType.mult
ADD = mybir.AluOpType.add
SIGMOID = mybir.ActivationFunctionType.Sigmoid

P = 128
PACK = 4
K_PASS = P * PACK
PASSES = K // K_PASS
BLOCKS = N // P
HALF_N = N // 2
HALF_J = J // 2
LIST_COLS = J // 16
RES_SCALE = 0.4
SHIFT_ROWS = 112


def tile_moe_one_expert_gates_another_kernel(tc, xt_words, xt_scales, wa_words, wa_scales, wb, res, offs, offs2, out):
    nc = tc.nc
    with ExitStack() as ctx:
        keep = ctx.enter_context(tc.tile_pool(name="keep", bufs=1))
        later = ctx.enter_context(tc.tile_pool(name="later", bufs=1))
        shared = ctx.enter_context(tc.tile_pool(name="shared", bufs=1))
        psum = ctx.enter_context(tc.psum_pool(name="psum", bufs=1))

        def sb(name, shape, dtype, tag=""):
            return keep.tile(shape, dtype, name=name, tag=tag or name, align_bytes=64)

        list_a = keep.tile([P, LIST_COLS], U16, name="list_a")
        list_b = keep.tile([P, LIST_COLS], U16, name="list_b")
        x_words = [sb("x_words%d" % z, [P, T], I32) for z in range(PASSES)]
        x_scales = sb("x_scales", [P, T], U8)
        wa_codes = sb("wa_codes", [P, PASSES, 2 * N], U8)
        wa_plane = sb("wa_plane", [P, PASSES, N], U8)
        xa_shifted = sb("xa_shifted", [P, J], U8)
        windows = [sb("window%d" % b, [P, T], F32) for b in range(2)]
        identity = sb("identity", [P, P], F32)
        warm = sb("warm", [P, 2], F32)

        nc.vector.memset(x_scales[:].bitcast(I32), 0)
        nc.vector.memset(warm[:, 0:1], 0.0)
        nc.vector.memset(xa_shifted[:].bitcast(I32), 0)
        nc.vector.memset(wa_plane[:].rearrange("p z n -> p (z n)").bitcast(I32), 0)
        nc.vector.memset(identity[:], 0.0)
        make_identity(nc, identity[:], nomemset=True)
        for w in windows:
            nc.vector.memset(w[:], 0.0)

        def words_src(z):
            return xt_words[z].rearrange("p c r -> p (c r)").bitcast(I32)

        wb_raw = {}

        def load_wb(b, z, raw):
            rows = wb[z * K_PASS : (z + 1) * K_PASS, b * P : b * P + raw.shape[2]]
            nc.sync.dma_start(raw[:], rows.rearrange("(p j) n -> p j n", j=PACK))
            wb_raw[b, z] = raw

        nc.sync.dma_start(list_a[:], offs)
        nc.sync.dma_start(list_b[:], offs2)
        for q in range(4):
            queue = nc.sync if q < 2 else nc.scalar
            queue.dma_start(
                x_scales[32 * q : 32 * q + 8, :].bitcast(I32),
                xt_scales[:, 4 * q : 4 * q + 4, :].bitcast(I32),
            )
        nc.sync.dma_start(x_words[0][:], words_src(0))
        for z in range(PASSES):
            load_wb(0, z, sb("wb_raw0%d" % z, [P, PACK, HALF_N], F32))
        nc.sync.dma_start(x_words[1][:], words_src(1))
        nc.scalar.activation(warm[:, 1:2], warm[:, 0:1], SIGMOID)
        nc.scalar.dma_start(
            wa_codes[:].bitcast(I32), wa_words.rearrange("z p c -> p z c").bitcast(I32)
        )
        for q in range(4):
            nc.scalar.dma_start(
                wa_plane[32 * q : 32 * q + 4, :, :].bitcast(I32),
                wa_scales[:, 4 * q : 4 * q + 4, :].rearrange("z r n -> r z n").bitcast(I32),
            )

        xa_words = [sb("xa_words%d" % z, [P, J], U32) for z in range(PASSES)]
        xb_words = [sb("xb_words%d" % z, [P, J], U32) for z in range(PASSES)]
        xa_scales = sb("xa_scales", [P, J], U8)
        xb_scales = sb("xb_scales", [P, J], U8)

        def gather_words(dst, z, lst, j0, j1):
            nc.vector.tensor_copy(dst, x_words[z][:].bitcast(U32).indirect(lst[:, j0 // 16 : j1 // 16]))

        wb_codes = {}
        wb_scales = {}

        def cast_wb(b, grouped):
            width = grouped.shape[1] // PASSES
            for z in range(PASSES):
                nc.scalar.copy(
                    grouped[:, z * width : (z + 1) * width, :].rearrange("p (c i) t -> p c t i", i=4),
                    wb_raw[b, z][:].rearrange("p t (c i) -> p c t i", i=4),
                )

        def quantize_wb(b, grouped):
            words = grouped.shape[1]
            width = words // PASSES
            codes = sb("wb_codes%d" % b, [P, words], U32)
            scales = sb("wb_scales%d" % b, [P, words], U8)
            nc.vector.quantize_mx(
                out=codes[:].bitcast(FP8X4),
                scales=scales[:],
                in_=grouped[:].rearrange("p n t -> p (n t)"),
            )
            for i in range(width // P):
                for z in range(PASSES):
                    cols = slice(z * width + i * P, z * width + (i + 1) * P)
                    wb_codes[b + i, z] = codes[:, cols]
                    wb_scales[b + i, z] = scales[:, cols]

        low = shared.tile([P, PASSES * HALF_N, PACK], BF16, name="wb_low", align_bytes=64, offset=3072)
        nc.vector.tensor_copy(xa_scales[:], x_scales[:].indirect(list_a[:]))
        nc.scalar.dma_start(
            xa_shifted[0:SHIFT_ROWS, :].bitcast(I32), xa_scales[4 : 4 + SHIFT_ROWS, :].bitcast(I32)
        )
        cast_wb(0, low)
        nc.vector.tensor_copy(xb_scales[:], x_scales[:].indirect(list_b[:]))
        gather_words(xa_words[0][:], 0, list_a, 0, J)
        gather_words(xb_words[0][:], 0, list_b, 0, J)
        quantize_wb(0, low)
        for j0 in (0, HALF_J):
            gather_words(xb_words[1][:, j0 : j0 + HALF_J], 1, list_b, j0, j0 + HALF_J)
            gather_words(xa_words[1][:, j0 : j0 + HALF_J], 1, list_a, j0, j0 + HALF_J)

        res_tiles = {}

        def load_res(b, tag):
            r = sb("res%d" % b, [P, T], F32, tag)
            nc.sync.dma_start(r[:], res[b * P : (b + 1) * P, :])
            res_tiles[b] = r

        load_res(0, "x_words0")
        load_res(1, "wb_raw00")
        load_wb(2, 0, shared.tile([P, PACK, P], F32, name="wb_raw20", align_bytes=64, offset=2048))
        load_wb(2, 1, sb("wb_raw21", [P, PACK, P], F32, "x_words1"))

        def gate_product(b, j0, j1, bank, gate):
            acc = psum.tile([P, J], F32, name="acc", tag=bank)
            for z in range(PASSES):
                nc.tensor.matmul_mx(
                    out=acc[:, 0 : j1 - j0],
                    lhsT=wb_codes[b, z].bitcast(FP8X4),
                    lhsT_scale=wb_scales[b, z],
                    rhs=xb_words[z][:, j0:j1].bitcast(FP8X4),
                    rhs_scale=xb_scales[4 * z : P, j0:j1],
                    start=(z == 0),
                    stop=(z == PASSES - 1),
                )
            nc.scalar.activation(gate, acc[:, 0 : j1 - j0], SIGMOID)

        def value_product(b, j0, j1, bank, value):
            acc = psum.tile([P, J], F32, name="acc", tag=bank)
            step = J if j1 - j0 == J else P
            for c0 in range(j0, j1, step):
                for z in range(PASSES):
                    plane = xa_scales if z == 0 else xa_shifted
                    nc.tensor.matmul_mx(
                        out=acc[:, c0 - j0 : c0 - j0 + step],
                        lhsT=wa_codes[:, z, 2 * b * P : 2 * (b + 1) * P].bitcast(FP4X4),
                        lhsT_scale=wa_plane[:, z, b * P : (b + 1) * P],
                        rhs=xa_words[z][:, c0 : c0 + step].bitcast(FP8X4),
                        rhs_scale=plane[:, c0 : c0 + step],
                        start=(z == 0),
                        stop=(z == PASSES - 1),
                    )
            if b < 2:
                nc.scalar.mul(value, acc[:, 0 : j1 - j0], 1.0 / RES_SCALE)
            else:
                nc.scalar.copy(value, acc[:, 0 : j1 - j0])

        def scatter(b, j0, j1, value, gate):
            nc.vector.tensor_tensor(
                windows[b % 3][:].indirect(list_a[:, j0 // 16 : j1 // 16]), value, gate, MULT
            )

        def finish(b, y, edges):
            for c in range(len(edges) - 1):
                cols = slice(edges[c], edges[c + 1])
                nc.vector.scalar_tensor_tensor(
                    y[:, cols], res_tiles[b][:, cols], RES_SCALE, windows[b % 3][:, cols], MULT, ADD
                )
                nc.sync.dma_start(out[b * P : (b + 1) * P, cols], y[:, cols])

        def add_turned(b, half, bank, staged):
            turned = psum.tile([P, J], F32, name="acc", tag=bank)
            for c in range(J // P):
                cols = slice(half * J + c * P, half * J + (c + 1) * P)
                for source, first in ((res_tiles[b], True), (windows[b % 3], False)):
                    nc.tensor.matmul(
                        turned[:, c * P : (c + 1) * P],
                        lhsT=source[:, cols],
                        rhs=identity[:],
                        start=first,
                        stop=not first,
                        is_transpose=True,
                    )
            nc.scalar.copy(staged, turned[:])

        def turn_back(b, half, bank, staged):
            back = psum.tile([P, J], F32, name="acc", tag=bank)
            for c in range(J // P):
                cols = slice(c * P, (c + 1) * P)
                nc.tensor.transpose(back[:, cols], staged[:, cols], identity[:])
            y = sb("y%d_%d" % (b, half), [P, J], F32)
            nc.scalar.mul(y[:], back[:], RES_SCALE)
            nc.scalar.dma_start(out[b * P : (b + 1) * P, half * J : (half + 1) * J], y[:])

        value = sb("value0_0", [P, HALF_J], F32)
        gate = later.tile([P, HALF_J], F32, name="gate0_0", align_bytes=64, offset=1536)
        gate_product(0, 0, HALF_J, "bank0", gate[:])
        value_product(0, 0, HALF_J, "bank1", value[:])
        scatter(0, 0, HALF_J, value[:], gate[:])
        windows.append(sb("window2", [P, T], F32, "value0_0"))
        nc.gpsimd.memset(windows[2][:], 0.0)
        for z in range(PASSES):
            load_wb(3, z, later.tile([P, PACK, P], F32, name="wb_raw3%d" % z, align_bytes=64, offset=2048 * z))
        gate = sb("gate0_256", [P, HALF_J], F32)
        gate_product(0, HALF_J, J, "bank3", gate[:])
        value = sb("value0_256", [P, HALF_J], F32, "wb_raw01")
        value_product(0, HALF_J, J, "bank5", value[:])
        scatter(0, HALF_J, J, value[:], gate[:])
        load_res(2, "wb_raw01")

        gate = sb("gate1", [P, J], F32)
        gate_product(1, 0, J, "bank4", gate[:])
        grouped = sb("wb_third", [P, PASSES * P, PACK], BF16)
        cast_wb(2, grouped)
        value = sb("value1", [P, J], F32, "x_words1")
        value_product(1, 0, J, "bank6", value[:])
        quantize_wb(2, grouped)
        scatter(1, 0, J, value[:], gate[:])
        load_res(3, "x_words1")

        gate = sb("gate2", [P, J], F32)
        gate_product(2, 0, J, "bank1", gate[:])
        grouped = sb("wb_fourth", [P, PASSES * P, PACK], BF16)
        cast_wb(3, grouped)
        value = later.tile([P, J], F32, name="value2", align_bytes=64, offset=2048)
        value_product(2, 0, J, "bank7", value[:])
        quantize_wb(3, grouped)
        scatter(2, 0, J, value[:], gate[:])

        late = sb("late", [P, 3 * J], F32, "wb_fourth")
        value = late[:, 0:J]
        value_product(3, 0, J, "bank0", value)
        add_turned(0, 0, "bank6", late[:, J : 2 * J])
        add_turned(0, 1, "bank1", late[:, 2 * J : 3 * J])
        gate = sb("gate3", [P, J], F32)
        gate_product(3, 0, J, "bank2", gate[:])
        turn_back(0, 0, "bank6", late[:, J : 2 * J])
        turn_back(0, 1, "bank1", late[:, 2 * J : 3 * J])
        finish(2, sb("y2", [P, T], F32), (0, T))
        scatter(3, 0, J, value, gate[:])
        staged = sb("staged1", [P, T], F32)
        add_turned(1, 0, "bank0", staged[:, 0:J])
        add_turned(1, 1, "bank2", staged[:, J:T])
        turn_back(1, 0, "bank0", staged[:, 0:J])
        turn_back(1, 1, "bank2", staged[:, J:T])
        finish(3, sb("y3", [P, T], F32), (0, T // 2, 3 * T // 4, T))
